import numpy as np, ml_dtypes
CORES = [48,51,52,55]
N = 4
BF = ml_dtypes.bfloat16
Y, X, O, S, Q, R = 64, 64, 1024, 4, 256, 6
PL = Y * X
def plain(rng):
    u = 0.5 - 0.5 * np.cos(np.pi * rng.random((N, 8, 16, O)))
    v = np.where((np.arange(8) % 2 == 0)[None, :, None, None], 0.25 + 3.75 * u, (0.5 + 1.5 * u) * np.exp2(rng.integers(-1, 2, (N, 8, 16, 1))))
    return v, rng.integers(0, 16, (N, 8, 16, O)), rng.integers(-7, 8, (N, 3, 128, 128))
def pack(v, z, a):
    a = a.astype(np.float32).astype(BF)
    return {"v0": np.ascontiguousarray(np.clip(v, 0.25, 4.0).reshape(N, 128, O)).astype(np.float32).astype(BF), "z0": np.ascontiguousarray(z.reshape(N, 128, O)).astype(np.float32).astype(BF),
            "ay": np.ascontiguousarray(a[:, 0]), "ax": np.ascontiguousarray(a[:, 1]), "bm": np.ascontiguousarray(a[:, 2])}
def slip():
    s0 = np.arange(208, 256) * 2.0 ** -6; e = np.repeat(s0[None, :], S, axis=0); b = e.copy()
    for t in range(R):
        p = t % S; o = (t - 1) % S
        e[p] = 0.5 * e[p] + 0.25 * np.exp(-np.minimum(0.125 * np.abs(e[p] - e[o]), 0.25)) * e[o]
        c = b.astype(np.float32).astype(BF).astype(np.float64)
        b[p] = 0.5 * b[p] + 0.25 * np.exp(-np.minimum(0.125 * np.abs(c[p] - c[o]), 0.25)) * b[o]
    return s0, np.max(np.abs(e - b), axis=0)
def setup_inputs(rng):
    return pack(*plain(rng))
def setup_inputs_spread(rng):
    v, z, a = plain(rng)
    v = (0.5 + 1.5 * rng.random((N, 8, 16, O))) * np.exp2(rng.integers(-1, 2, (N, 8, 1, O)))
    z = np.minimum((16 * rng.random((N, 8, 16, O)) ** rng.choice(np.array([0.25, 1.0, 4.0]), (N, 8, 16, 1))).astype(np.int64), 15)
    cap = rng.integers(1, 8, (N, 3, 1, 128)); share = rng.choice(np.array([0.2, 0.6, 1.0]), (N, 3, 1, 128))
    a = np.clip(a, -cap, cap) * (rng.random(a.shape) < share)
    return pack(v, z, a)
def setup_inputs_ends(rng):
    base = rng.random((1, 8, 16, 1)) < 0.5
    flip = (rng.random((N, 8, 16, O)) < 1 / 8) ^ (rng.random((N, 8, 1, O)) < 1 / 16)
    flip[:, :, :, 0] = False; flip[:, :, :, O - 1] = True
    v = np.where(base ^ flip, 4.0, 0.25)
    full = np.array([0, O // 2 + 1, O - 2, O - 1]); less = np.array([2, 3, 4, 5, O - 5, O - 4])
    dens = rng.choice(np.array([0, 1 / 32, 1 / 8, 1.0]), (N, 1, 1, O), p=np.array([0.05, 0.55, 0.36, 0.04])); dens[..., full] = 1.0; dens[..., np.array([1, O - 3])] = 0.0; dens[..., less] = 1.0
    z = 15 * (rng.random((N, 8, 16, O)) < dens)
    m = np.where((dens == 1.0) & (rng.random(dens.shape) < 0.5), rng.integers(1, 41, dens.shape), 0); m[..., full] = 0; m[..., less] = 1
    z = np.where(np.argsort(rng.random((N, 128, O)), axis=1).reshape(N, 8, 16, O) < m, 0, z)
    a = rng.choice(np.array([-7, 7]), (N, 3, 128, 128))
    a[:, :2, :, 5::16] = np.where(np.argsort(rng.random((N, 2, 128, 8)), axis=2) < 64, 7, -7)
    a[:, 0, :, 127] = 7; a[:, 1, :, 127] = -7; a[:, 0, :, 0] = -7; a[:, 1, :, 0] = 7; a[:, :2, :, 50] = 7; a[:, :2, :, 81] = -7
    a[:, 2, :, 127] = 7; a[:, 2, :, 126] = -7; a[:, 2, :, 1] = 7; a[:, 2, :, 64] = -7
    return pack(v, z, a)
def setup_inputs_near(rng):
    v, z, a = plain(rng)
    cand = np.arange(60, 340); w = np.exp(-cand * 2.0 ** -13); off = np.abs(w - w.astype(np.float32).astype(BF).astype(np.float64))
    n = rng.choice(cand[np.argsort(-off)[:24]], 8)[:, None]
    mag = rng.integers(80, 112, (8, 16)); dif = (n // 16 + (np.arange(16)[None, :] < n % 16)) * rng.choice(np.array([-1, 1]), (8, 16))
    half = ((np.arange(8) // 2 + int(rng.integers(0, 2))) % 2 == 1)[:, None]
    far = half & (np.argsort(rng.random((8, 16)), axis=1) < 14); i = rng.integers(0, 25, (8, 16)); j = rng.integers(0, 8, (8, 16))
    one = np.where(far, (388 + 2 * i + 4 * j) * 2.0 ** -7, mag * 2.0 ** -6)
    two = np.where(far, (129 + 2 * i) * 2.0 ** -7, np.where(half, mag, mag + dif) * 2.0 ** -6)
    share = np.where(np.arange(8) % 2 == 0, 0.5, 0.1)[None, :, None, None]
    kind = rng.random((N, 8, 1, O)) < share
    v = np.where(kind, two[None, :, :, None], one[None, :, :, None])
    for g in np.flatnonzero(half): a[:, 1, :, 16 * g:16 * g + 16] = 0
    return pack(v, z, a)
def setup_inputs_corners(rng):
    v, z, a = plain(rng); sh = int(rng.integers(0, 8)); i16 = np.arange(16)
    for g in range(8):
        k = (g + sh) % 8; lo = 16 * g; hi = lo + 16; at = 16 * ((g + 3) % 8)
        if k == 0: v[:, g] = 0.25 + 0.0625 * v[:1, g, :, :1]
        elif k == 1: v[:, g] = 0.25
        elif k == 2: v[:, g] = np.where((rng.random((N, 1, O)) < 0.5) ^ (rng.random((1, 16, 1)) < 0.5), 1.0, 0.25)
        elif k == 3: v[:, g] = 0.25 + 0.1875 * v[:, g]; v[:, g, 1:] = 0.25
        else: v[:, g] = 1.0 + rng.random((N, 16, O))
        for q in range(N):
            c = (g + q + sh) % 8
            if c == 0: a[q, :2, :, lo:hi] = 0
            elif c == 1: a[q, :2, :, lo:hi] = a[q, :2, :, lo:lo + 1].copy()
            elif c == 2 or c == 3:
                a[q, :2, :, lo:hi] = 0
                for j in range(2): a[q, j, rng.integers(0, 128, 16), lo + i16] = -1 if c == 2 else 1
            elif c == 4: a[q, 0, :, lo:hi] = 0
            elif c == 5: a[q, 1, :, lo:hi] = 0
            elif c == 6:
                w = (1 + (q // 2) % (N - 1)) * (O // X)
                a[q, 0, :, lo:hi] = 0; a[q, 0, at:at + 16, lo:hi] = (w // 16 + (i16 < w % 16))[:, None]
            else:
                a[q, :2, :, lo:hi] = 0; a[q, 1, at:at + 12, lo:hi] = -7; a[q, 0, at + 12:at + 16, lo:hi] = -7
            e = (c + 3) % 8
            if e == 0: z[q, g] = 0
            elif e == 1: z[q, g] = 15
            elif e == 2: z[q, g] = rng.integers(7, 9, (16, O))
            elif e == 3: z[q, g] = rng.integers(0, 2, (16, O))
            elif e == 4:
                z[q, g] = 8
                if q % 2 == 1: z[q, g, :, S * int(rng.integers(0, Q)):][:, :S] = 0
            elif e == 5:
                nx = 8 * (np.arange(O) % X + q % 2) // 7; ny = 8 * (np.arange(O) // X + q % 2) // 7
                z[q, g, :12] = nx[None, :] // 12 + (np.arange(12)[:, None] < nx[None, :] % 12)
                z[q, g, 12:] = ny[None, :] // 4 + (np.arange(4)[:, None] < ny[None, :] % 4)
            b = (c + 6) % 8
            if b == 0: a[q, 2, :, lo:hi] = 0
            elif b == 1 or b == 2:
                a[q, 2, :, lo:hi] = 0; a[q, 2, rng.integers(0, 128, 16), lo + i16] = 1 if b == 1 else -1
            elif b == 3: a[q, 2, :, lo:hi] = 7
    return pack(v, z, a)
def setup_inputs_calm(rng):
    v, z, a = plain(rng); sh = int(rng.integers(0, 8)); i16 = np.arange(16); a[:, 2] = 0
    lev = np.ones(S)
    for t in range(R): lev[t % S] = 0.5 * lev[t % S] + 0.25 * np.mean(lev)
    v = 0.285 / np.sqrt(np.mean(lev * lev)) * (0.8 + 0.4 * rng.random((N, 8, 16, O)))
    s0, far = slip(); alike = float(rng.choice(s0[np.argsort(-far)[:6]]))
    owner = int(rng.integers(0, N)); pick = (np.arange(O) // S) % 16 == int(rng.integers(0, 16)); at = 16 * ((7 - sh) % 8); st = O // X
    for g in range(8):
        h = (g + sh) % 8; lo = 16 * g; hi = lo + 16
        for q in range(N): a[q, 2, lo + (i16 if h == 7 else rng.integers(0, 16, 16)), lo + i16] = 1 if h < 4 else 4
        u = rng.random((N, 16, O))
        if h < 4: z[:, g] = rng.integers(4 * h, 4 * h + 4, (N, 16, O))
        elif h < 6: z[:, g] = np.where(u < 0.0625, 15, np.where(u < 0.75, 14, 13))
        elif h == 6: z[:, g] = np.where(u < 0.01, 3, np.where(u < 0.03, 2, np.where(u < 0.08, 1, 0)))
        else: z[:, g] = 8 * ((i16[:, None] < 10) | pick[None, :])
        if h in (0, 1, 2, 7): a[:, :2, :, lo:hi] = 0
        for q in range(N):
            if h == 0:
                v[q, g] = 4.0 if q % 2 == 0 else 0.25
                if q % 2 == 1: a[q, 0, at + 10:at + 16, lo:hi] = (st // 6 + (np.arange(6) < st % 6))[:, None]
            elif h == 1:
                w = ((owner - q) % N) * st
                if 2 * w > Y: w = w - Y
                a[q, 0, at:at + 10, lo:hi] = (w // 10 + (np.arange(10) < w % 10))[:, None]
                a[q, 1, at:at + 10, lo:hi] = np.arange(10)[:, None] < (i16 % S)[None, :]
            elif h == 2 and q % 2 == 0:
                v[q, g] = alike; a[q, 1, at, lo:hi] = -1
    return pack(v, z, a)
def check_ranges(d):
    bad = []
    for k, lo, hi, w in (("v0", 0.25, 4, False), ("z0", 0, 15, True), ("ay", -7, 7, True), ("ax", -7, 7, True), ("bm", -7, 7, True)):
        a = np.asarray(d[k]).astype(np.float32)
        if not np.all((a >= lo) & (a <= hi)): bad.append("range of " + k)
        elif w and np.any(a != np.floor(a)): bad.append("whole numbers in " + k)
    return bad
def reference(v0, z0, ay, ax, bm):
    V = np.ascontiguousarray(v0.astype(np.float64).transpose(1, 0, 2)).reshape(8, 16, PL)
    z = np.ascontiguousarray(z0.astype(np.float32).astype(np.int64).transpose(1, 0, 2)).reshape(8, 16, PL)
    cy, cx, cb = [a.astype(np.float32).astype(np.int64).transpose(0, 2, 1) for a in (ay, ax, bm)]
    for t in range(R):
        nv = V.copy(); nz = z.copy()
        for r in range(N):
            own = r * O + S * np.arange(Q) + t % S
            zq = z.reshape(128, PL)[:, own]; vq = V[:, :, own]
            dy = np.matmul(cy[r], zq) >> 3; dx = np.matmul(cx[r], zq) >> 3
            pl = X * ((own // X + dy) & (Y - 1)) + ((own % X + dx) & (X - 1))
            ix = pl.reshape(8, 1, 16 * Q)
            m = np.max(np.take_along_axis(z, ix, 2).reshape(8, 16, 16, Q), axis=2).reshape(128, Q)
            nz[:, :, own] = ((np.matmul(cb[r], m) >> 2) & 15).reshape(8, 16, Q)
            vs = np.take_along_axis(V, ix, 2).reshape(8, 16, 16, Q)
            d = np.minimum(0.0078125 * np.sum(np.abs(vq[:, :, None, :] - vs), axis=1), 0.25)
            nv[:, :, own] = 0.5 * vq + 0.015625 * np.sum(np.exp(-d)[:, None] * vs, axis=2)
        V, z = nv, nz
    return {"yv": np.ascontiguousarray(V.reshape(128, N, O).transpose(1, 0, 2)).astype(np.float32), "yz": np.ascontiguousarray(z.reshape(128, N, O).transpose(1, 0, 2)).astype(np.float32)}

def check_inputs(d):
    bad = list(check_ranges(d))
    if not bad:
        for name, y in reference(**d).items():
            for q in range(N):
                v = np.abs(np.asarray(y[q], np.float64)); s = np.sqrt(np.mean(v * v))
                if v.max() > 5 * s or s < 2.0 ** -3: bad.append('%s of rank %d is uneven or too small' % (name, q))
    return bad

import math
from concourse.bass import DstId, RemoteDMATransfer
from concourse.mybir import AluOpType, ActivationFunctionType

LAYERS = 6
SCRATCH = {
    "VN": ("sbuf", [128, 1024], "bfloat16"), "ZN": ("sbuf", [128, 1024], "bfloat16"),
    "MA": ("sbuf", [128, 384], "bfloat16"),
    "VB": ("sbuf", [128, 4096], "bfloat16"), "VT": ("sbuf", [128, 8192], "float32"),
    "ZT": ("sbuf", [128, 9216], "bfloat16"),
    "D": ("sbuf", [128, 4096], "float32"), "AB": ("sbuf", [128, 4096], "float32"),
    "ST": ("sbuf", [128, 4096], "float32"),
    "ZG": ("sbuf", [128, 4096], "bfloat16"), "ZS": ("sbuf", [128, 4096], "bfloat16"),
    "R0": ("sbuf", [128, 4096], "bfloat16"), "R1": ("sbuf", [128, 4096], "bfloat16"),
    "R2": ("sbuf", [128, 4096], "bfloat16"), "R3": ("sbuf", [128, 4096], "bfloat16"),
    "R4": ("sbuf", [128, 4096], "float32"), "R5": ("sbuf", [128, 4096], "float32"),
    "IDX": ("sbuf", [128, 1536], "uint16"),
    "YV": ("sbuf", [128, 1024], "float32"), "YZ": ("sbuf", [128, 1024], "float32"),
    "U": ("sbuf", [128, 512], "float32"), "W": ("sbuf", [128, 256], "float32"),
    "HI": ("sbuf", [128, 512], "bfloat16"), "X": ("sbuf", [128, 512], "float16"),
    "CM": ("sbuf", [128, 256], "float32"), "T2": ("sbuf", [128, 256], "float32"),
    "F0": ("sbuf", [128, 1536], "bfloat16"), "F1": ("sbuf", [128, 1536], "bfloat16"),
    "F2": ("sbuf", [128, 1536], "bfloat16"), "F3": ("sbuf", [128, 1536], "bfloat16"),
    "ZF": ("sbuf", [128, 768], "bfloat16"),
    "JP": ("sbuf", [128, 128], "float32"), "EYE": ("sbuf", [128, 512], "bfloat16"),
    "DM": ("sbuf", [128, 128], "float32"), "CX": ("sbuf", [128, 128], "float32"),
    "MK": ("sbuf", [128, 128], "float32"), "BL": ("sbuf", [128, 256], "float32"),
    "BK": ("sbuf", [128, 16], "float32"), "SEL": ("sbuf", [128, 1024], "float16"),
    "ROW": ("sbuf", [128, 1024], "bfloat16"), "RQ": ("sbuf", [128, 64], "bfloat16"),
    "PI": ("sbuf", [128, 8], "int32"), "CI": ("sbuf", [128, 8], "int32"),
    "CF": ("sbuf", [128, 8], "float32"), "CG": ("sbuf", [128, 8], "float32"),
    "ZM": ("sbuf", [128, 1024], "bfloat16"),
    "CY": ("sbuf", [128, 256], "bfloat16"), "CXR": ("sbuf", [128, 1024], "bfloat16"),
    "ONE": ("sbuf", [128, 128], "bfloat16"), "NEG": ("sbuf", [128, 256], "bfloat16"),
}
for _b in range(8):
    SCRATCH["P%d" % _b] = ("psum", [128, 512], "float32")
SEMAPHORES = (["cV", "cA", "cP", "cG", "sent", "outs", "cast", "ldv", "ldz", "ld0", "ld1", "ld2"]
              + ["vin%d" % t for t in range(LAYERS)] + ["zin%d" % t for t in range(LAYERS)])
OPT = {"zfirst": True, "zdve": [3, 1, 1, 1, 1, 1], "vsend": [[0, 1, 2], [3]], "gsplit": [2, 2, 2, 2], "asplit": [2, 2, 2, 2], "zsplit": [2, 2, 2, 2],
       "onv": [], "onv0": []}
ORDER = "00021o01031p041m0l0k1q1r1n0o0j0q0p0i180x170m0n0v0u16100y190z1a070806051s2p281t0w111b091d0r291c130s1u12142q0t1f361i1k1w1l2a1g1j151h1v1e370b1x2d2c0d2r0c1z0e202b211y0f382322272e2s2426250a2t62615z2u3b2v5v5w2f5s5t2g0g5y3a5x63395u60643c2h0h2i3n2j65662k3p3q3o3y6768693r3s6a6b6c3z4m4n406d3t3u4241432l3v3w3x2w4e4g4x4y4o44454q494p2m4r47464a2n483d4z4s4f4i512o4b4h4t8y52504k4u4v534c4j4w5d545f8z5856554l594d915e575k5a5b5m5g92945l5h2x5c5i5j5n955o5p9893979996905q9a9b9c9e9d5r2y2z6t306u319f6v6w6x6y7476779g9h9i756z707s78327271797t737u7a7k7m7b7w7f3383847v7x7d7c7g7e7o34857y7z867l87357h7n88c5817q7i7p8089828j8a8lc68e7r8f8c8b7jc88k8d8q8g8h8s8m6e6fc9cb8r3e6h8n8i8o8p8tcc8u8v8w8xce6gc7cfcacdcg3f3gch6icicja1a4ckcla0aba53h3icma2a3ac6jcn9jcocpada6a7aeazaf3ja8agb0a9aaatarb1ahaib3amb23kb4babbajakalan3lbcb5bdb6avasbe3maoauexb8bfaxapawb7bgb9bqbhbseyayblbmaqbjbi9kf1brbkbxbnbobzbt9lf4f0bybpbu6kf39n9obvbwc0c1c2c3c4f7ezf5f2f69mf8f9fafb6lfcfd6m9pcs6n6ofecucvctcwcxd3d5fffgfhd4cyd6czdrd76pd1d8dsd0d2dldj9qdtd9dadvdedu6qdwe2e3dcdbdf6rdde4dxdndydke6dze0dpe5e7dme16sdghpdhe8doeie9ekcqcrdqedeeebeadihsejecepefeghqerelhthveq9remeheneoeshweteuhrhuhzhxhyi0evew9si1i2i3i59t9ufl9vi4i6fofpfkfmfnfvfxfyi7i8i9fwfqfrgjfzfsft9wg0gkfuglgvg1gbgdg2g6gn9xgugmgog4g3g7g5gf9ygwgcgpgxgqgygsgrgz9zg8gegggtghg9h0hah1kghcfifjgih5h6gah2h3kjhbh4khhhh7h8hjhdkkkmhih9hehfhghkknhlhmhnhokpklkqkikskoktkukrl0l1ickvl2idkwkxieifigihinl3ipl4l5ioiiijiqjbirisjcilikimj5j3jditiujfiyjmjnjeiwivixjgizj7jojhj4jqj9jij6j0jrjpj8jjjkjliakyjsjxjakzk2ibj1jyk4jtjujvk3jzj2k0l6k5jwl7k9kbk6k1k7k8kakckdkekf"


def v(name, c0, c1, step=1, p0=0, p1=128):
    return ("v", name, p0, p1, c0, c1, step)


def ind(win, off):
    return ("i", win, off)


def isview(a):
    return isinstance(a, tuple) and a[0] in ("v", "i")


def count(a):
    if a[0] == "i":
        return 16 * count(a[2])
    return (a[5] - a[4] + a[6] - 1) // a[6]


def spans(a):
    if a[0] == "i":
        return spans(a[1]) + spans(a[2])
    return [(a[1], a[4], a[4] + (count(a) - 1) * a[6] + 1)]


def kind(a):
    return SCRATCH[a[1]][2]


def plan(r):
    ops = []
    A, Fn = AluOpType, ActivationFunctionType

    def add(eng, call, args, outs, kw=None, **more):
        rd = [s for i, a in enumerate(args) if isview(a) and i not in outs for s in spans(a)]
        for a in (kw or {}).values():
            if isview(a):
                rd += spans(a)
        o = {"eng": eng, "call": call, "args": args, "kw": kw or {}, "rd": rd, "outs": [args[i] for i in outs],
             "after": []}
        o.update(more)
        ops.append(o)
        return len(ops) - 1

    def ts(out, in0, s1, s2, *op):
        return add("V", "tensor_scalar", [out, in0, s1, s2] + list(op), [0])

    def tt(out, a, b, op):
        return add("V", "tensor_tensor", [out, a, b, op], [0])

    def cp(out, a):
        return add("V", "tensor_copy", [out, a], [0])

    def ms(out, c):
        return add("V", "memset", [out, c], [0])

    def scan(out, a, b, op):
        return add("V", "tensor_tensor_scan", [out, a, b, 0.0, A.mult, op], [0])

    def act(out, a, f, bias=None, scale=None):
        kw = {}
        if bias is not None:
            kw["bias"] = bias
        if scale is not None:
            kw["scale"] = scale
        return add("A", "activation", [out, a, f], [0], kw)

    def aff(out, a, scale, bias, on_vector):
        if on_vector:
            return ts(out, a, scale, bias, A.mult, A.add)
        return act(out, a, Fn.Identity, bias, scale)

    def mm(*groups):
        i = add("P", "matmul", list(groups), [])
        ops[i]["outs"] = [out for out, terms in groups]
        ops[i]["rd"] = [s for out, terms in groups for term in terms for a in term for s in spans(a)]
        return i

    def iota(out, pat, base, cm):
        kw = {} if kind(out) == "int32" else {"allow_small_or_imprecise_dtypes": True}
        return add("G", "iota", [out, pat, base, cm], [0], kw)

    def gcp(out, a):
        return add("G", "affine_select", [out, a, [[0, count(a)]], A.is_ge, 0.0, 0, 0], [0])

    def arrive(sends, sem, name, starts):
        outs = [v(name, s + 256 * q, s + 256 * q + 256) for s in starts for q in range(4) if q != r]
        i = add("X", "arrive", [], [], after=list(sends), sem=sem, val=48 * len(sends))
        ops[i]["outs"] = outs
        return i

    own = 256 * r

    def vslot(s, c0, c1):
        return v("VT", 1024 * (s - 1) + c0, 1024 * (s - 1) + c1)

    def vq(t, c0, c1):
        return v("VB", 1024 * t + own + c0, 1024 * t + own + c1) if t < 4 else vslot(t, own + c0, own + c1)

    both = [("v0", "VN", "VB", "ldv", "vin0"), ("z0", "ZN", "ZT", "ldz", "zin0")]
    if OPT["zfirst"]:
        both.reverse()
    add("S", "load", [v(both[0][1], 0, 1024)], [0], src=both[0][0], sem=both[0][3])
    add("S", "load", [v(both[1][1], 0, 1024)], [0], src=both[1][0], sem=both[1][3], after=[0], loose=True)
    for i, nm in enumerate(("ay", "ax", "bm")):
        add("A", "load", [v("MA", 128 * i, 128 * i + 128)], [0], src=nm, sem="ld%d" % i)
    before = []
    for src, raw, table, ld, sem in both:
        for ph in range(4):
            cp(v(table, 1024 * ph + own, 1024 * ph + own + 256), v(raw, ph, 1024, 4))
        before = [add("G", "send", [v(table, 1024 * ph + own, 1024 * ph + own + 256) for ph in range(4)], [],
                      sem=sem, after=before)]
        s = arrive(before, sem, table, [0, 1024, 2048, 3072])
    add("G", "cast", [v("VT", 0, 3072), v("VB", 1024, 4096)], [0], sem="cast", after=[s])

    iota(v("PI", 0, 1), [[0, 1]], 0, 1)
    iota(v("JP", 0, 128), [[1, 128]], 0, -1)
    iota(v("CY", 0, 256, 1, 0, 1), [[8, 16], [0, 16]], 128 * r, 0)
    iota(v("CXR", 0, 256, 1, 0, 1), [[0, 16], [32, 16]], 0, 0)
    iota(v("ROW", 0, 128), [[1, 8], [0, 16]], 0, 0)
    iota(v("RQ", 0, 64), [[0, 8], [1, 8]], 0, 0)
    for ph in range(1, 4):
        ts(v("CXR", 256 * ph, 256 * ph + 256, 1, 0, 1), v("CXR", 0, 256, 1, 0, 1), 8.0 * ph, None, A.add)
    for n in (128, 256, 512):
        ts(v("ROW", n, 2 * n), v("ROW", 0, n), n / 16.0, None, A.add)
    cols = [(4, None), (None, 7), (1, None), (None, 1), (None, 15), (3, 7), (6, None)]
    for i, (sh, mask) in enumerate(cols):
        if sh is None:
            ts(v("CI", i, i + 1), v("PI", 0, 1), mask, None, A.bitwise_and)
        elif mask is None:
            ts(v("CI", i, i + 1), v("PI", 0, 1), sh, None, A.arith_shift_right)
        else:
            ts(v("CI", i, i + 1), v("PI", 0, 1), sh, mask, A.arith_shift_right, A.bitwise_and)
    cp(v("CF", 0, 7), v("CI", 0, 7))
    pg, p8, ph1, p3, upper = v("CF", 0, 1), v("CF", 1, 2), v("CF", 2, 3), v("CF", 5, 6), v("CF", 6, 7)
    sg, hb, k15, lower = v("CG", 0, 1), v("CG", 1, 2), v("CG", 2, 3), v("CG", 3, 4)
    ts(sg, v("CF", 3, 4), 2.0, -1.0, A.mult, A.add)
    ts(hb, v("CF", 3, 4), 100.0, -100.0, A.mult, A.add)
    ts(k15, v("CF", 4, 5), 15.0, None, A.is_equal)
    ts(lower, upper, 0.0, None, A.is_equal)
    eyes = [v("EYE", 128 * i, 128 * i + 128) for i in range(4)]
    eye = eyes[0]
    for i, f in enumerate((1.0, 16.0, 1024.0, -4096.0)):
        ts(eyes[i], v("JP", 0, 128), 0.0, f, A.is_equal, A.mult)
    ts(v("DM", 0, 128), v("JP", 0, 128), 1.0, None, A.is_equal)
    tt(v("DM", 0, 128), v("DM", 0, 128), eye, A.subtract)
    ms(v("DM", 0, 128, 16), 0.0)
    ts(v("BK", 0, 16), v("ROW", 0, 128, 8), pg, None, A.is_equal)
    for h in range(2):
        ts(v("BL", 128 * h, 128 * h + 128), v("ROW", 0, 128), p8, (lower, upper)[h], A.is_equal, A.mult)
        ts(v("SEL", 512 * h, 512 * h + 512), v("ROW", 512 * h, 512 * h + 512), ph1, sg, A.is_equal, A.mult)
        ts(v("MK", 64 * h, 64 * h + 64), v("ROW", 0, 128, 2), p3, None, A.is_equal)
    ts(v("CX", 0, 64), v("RQ", 0, 64), pg, None, A.is_equal)
    ts(v("CX", 64, 128), v("RQ", 0, 64), pg, k15, A.is_equal, A.mult)
    ms(v("ZM", 0, 1024), 1.0)
    ms(v("ZM", 0, 1024, 16), 0.0)
    one = v("ONE", 0, 128, 1, 0, 1)
    ms(one, 1.0)
    ms(v("NEG", 0, 256, 1, 0, 1), 0.0)
    ms(v("NEG", 0, 128, 16, 0, 1), -100.0)
    ms(v("NEG", 128, 192, 1, 0, 1), 0.5)

    def index(t):
        ph = t % 4
        onv = OPT["onv0"] if t < 4 else OPT["onv"]
        zq = v("ZN", ph, 1024, 4) if t < 4 else v("ZT", 1024 * t + own, 1024 * t + own + 256)
        bank = ("P6", "P0", "P1", "P2", "P6", "P6")[t]
        F = "F%d" % (t % 4)
        py, px = v(bank, 0, 256), v(bank, 256, 512)
        ty = [(v("MA", 0, 128), zq), (one, v("CY", 0, 256, 1, 0, 1))]
        tx = [(v("MA", 128, 256), zq), (one, v("CXR", 256 * ph, 256 * ph + 256, 1, 0, 1))]
        mm((py, ty), (px, tx))
        aff(v(F, 0, 512), v(bank, 0, 512), -1.0, -98048.5, "ih" in onv)
        mm((py, ty + [(eye, v(F, 0, 256))]), (px, tx + [(eye, v(F, 256, 512))]))
        aff(v(F, 512, 1024), v(bank, 0, 512), 0.125, 12479.5625, "i3" in onv)
        aff(v(F, 1024, 1280), px, 0.03125, 3263.515625, "i5" in onv)
        last = v(F, 1024, 1280)
        if ph:
            last = v(F, 1280, 1536)
            aff(last, px, 0.03125, 3263.515625 - 0.25 * ph, "i5" in onv)
        mm((py, [(eyes[1], v(F, 512, 768)), (eyes[2], v(F, 768, 1024)), (eye, v(F, 1024, 1280)), (eyes[3], last)]))
        ts(v("IDX", 256 * t, 256 * t + 256), py, 586560.0 - 1024.0 * ph, None, A.add)

    def repeat(t, f):
        R = "R%d" % t
        src = v("VN", t, 1024, 4) if t < 4 else vq(t, 0, 256)
        f(v(R, 0, 4096, 16), src)
        f(v(R, 8, 4096, 16), src)
        f(v(R, 4, 4096, 8), v(R, 0, 4096, 8))
        for h in range(2):
            f(v(R, 2048 * h + 2, 2048 * h + 2048, 4), v(R, 2048 * h, 2048 * h + 2048, 4))
        for h in range(4):
            f(v(R, 1024 * h + 1, 1024 * h + 1024, 2), v(R, 1024 * h, 1024 * h + 1024, 2))

    index(0)
    repeat(0, cp)
    for t in range(1, 4):
        index(t)
        repeat(t, gcp)
    lnk = -0.25 - math.log(64.0)
    ring = [0]
    for t in range(LAYERS):
        vwin = v("VB", 0, 4096) if t == 0 else v("VT", 1024 * (t - 1), 1024 * (t - 1) + 4096)
        zwin = v("ZT", 1024 * t, 1024 * t + 4096)

        def offs(a0, n):
            return v("IDX", 256 * t + a0 // 16, 256 * t + (a0 + n) // 16)

        sends = []
        for pair in range(2):
            for p in (2 * pair, 2 * pair + 1):
                e0, b, bank = 1024 * p, 128 * p, "P%d" % (4 + p % 2)
                n = 1024 // OPT["gsplit"][p]
                for a0 in range(e0, e0 + 1024, n):
                    tt(v("D", a0, a0 + n), ind(vwin, offs(a0, n)), v("R%d" % t, a0, a0 + n), A.subtract)
                n = 1024 // OPT["asplit"][p]
                for a0 in range(e0, e0 + 1024, n):
                    act(v("AB", a0, a0 + n), v("D", a0, a0 + n), Fn.Abs)
                    mm(*[(v(bank, (c - e0) // 8, (c - e0) // 8 + 16), [(v("AB", c, c + 128), v("BK", 0, 16))])
                         for c in range(a0, a0 + n, 128)])
                u, dl, o1 = v("U", b, b + 128), v(bank, 128, 256), v(bank, 256, 384)
                act(u, v(bank, 0, 128), Fn.Relu, 0.25, -0.0078125)
                mm((dl, [(u, v("DM", 0, 128)), (one, v("NEG", 0, 128, 1, 0, 1))]))
                act(v("HI", b, b + 128), dl, Fn.Exp)
                act(o1, dl, Fn.Exp, hb)
                tt(v("X", b, b + 128), o1, v("HI", b, b + 128), A.subtract)
            q0, q1 = 128 * pair, 128 * pair + 128
            act(v("W", q0, q1), v("U", 2 * q0 + 1, 2 * q1, 2), Fn.Exp, lnk)
            mm((v("P3", 256, 384), [(v("W", q0, q1), v("CX", 0, 128)), (one, v("NEG", 128, 256, 1, 0, 1))]))
            tt(v("CM", q0, q1), v("P3", 256, 384), v("MK", 0, 128), A.mult)
            mm(*[(v("P7", 256 * j + q0 + 64 * h, 256 * j + q0 + 64 * h + 64),
                  [(v("BL", 128 * h, 128 * h + 128), v("CM", q0 + 64 * j, q0 + 64 * j + 64))])
                 for j in range(2) for h in range(2)])
            tt(v("T2", q0, q1), v("P7", q0, q1), vq(t, q0, q1), A.mult)
            for p in (2 * pair, 2 * pair + 1):
                for h in range(2):
                    a0 = 1024 * p + 512 * h
                    bank = "P%d" % (ring[0] % 3)
                    ring[0] += 1
                    mm(*[(v(bank, 128 * c, 128 * c + 128),
                          [(v("SEL", 512 * h + 128 * c, 512 * h + 128 * c + 128), v("X", 128 * p, 128 * p + 128))])
                         for c in range(4)])
                    scan(v("ST", a0, a0 + 512), v(bank, 0, 512), v("D", a0, a0 + 512), A.add)
                for grp in OPT["vsend"]:
                    if grp[-1] != p:
                        continue
                    q0, q1 = 64 * grp[0], 64 * p + 64
                    c2 = v("P7", 256 + q0, 256 + q1)
                    tt(c2, c2, v("ST", 16 * q0 + 15, 16 * q1, 16), A.mult)
                    if t < 5:
                        tt(vslot(t + 4, own + q0, own + q1), c2, v("T2", q0, q1), A.add)
                        sends.append(add("G", "send", [vslot(t + 4, own + q0, own + q1)], [], sem="vin%d" % (t + 1)))
                    else:
                        tt(v("YV", 4 * q0 + 1, 4 * q1, 4), c2, v("T2", q0, q1), A.add)
                        add("S", "store", [v("YV", 4 * q0, 4 * q1)], [], dst="yv", sem="outs")
        if t < 5:
            arrive(sends, "vin%d" % (t + 1), "VT", [1024 * (t + 3)])
        for p in range(4):
            n = 1024 // OPT["zsplit"][p]
            for a0 in range(1024 * p, 1024 * p + 1024, n):
                if a0 >= 4096 - 512 * OPT["zdve"][t]:
                    cp(v("ZG", a0, a0 + n), ind(zwin, offs(a0, n)))
                else:
                    act(v("ZG", a0, a0 + n), ind(zwin, offs(a0, n)), Fn.Copy)
            scan(v("ZS", 1024 * p, 1024 * p + 1024), v("ZM", 0, 1024), v("ZG", 1024 * p, 1024 * p + 1024), A.max)
        onv = OPT["onv"]
        for q0, q1 in ([(0, 256)] if t < 5 else [(0, 128), (128, 256)]):
            pb = v("P3", q0, q1)
            mix = (v("MA", 256, 384), v("ZS", 16 * q0 + 15, 16 * q1, 16))
            f0, f1, f2 = [v("ZF", 256 * j + q0, 256 * j + q1) for j in range(3)]
            mm((pb, [mix]))
            aff(f0, pb, -1.0, -49024.5, "zh" in onv)
            mm((pb, [mix, (eye, f0)]))
            aff(f1, pb, 0.25, 12479.625, "z4" in onv)
            aff(f2, pb, -0.25, -15352.125, "z6" in onv)
            mm((pb, [(eye, f1), (eye, f2)]))
            if t == 5:
                aff(v("YZ", 4 * q0 + 1, 4 * q1, 4), pb, 1.0, 2880.0, "zf" in onv)
                add("S", "store", [v("YZ", 4 * q0, 4 * q1)], [], dst="yz", sem="outs")
        if t < 5:
            zn = v("ZT", 1024 * (t + 4) + own, 1024 * (t + 4) + own + 256)
            aff(zn, pb, 1.0, 2880.0, "zf" in onv)
            arrive([add("G", "send", [zn], [], sem="zin%d" % (t + 1))], "zin%d" % (t + 1), "ZT", [1024 * (t + 4)])
            if t >= 2:
                gcp(v("YZ", t % 4, 1024, 4), zn)
                gcp(v("YV", t % 4, 1024, 4), vslot(t + 4, own, own + 256))
            if t < 2:
                index(t + 4)
                repeat(t + 4, gcp)

    wlast, rlast = {}, {}
    for i, o in enumerate(ops):
        wr = [s for a in o["outs"] for s in spans(a)]
        d = set(o["after"])
        if o["call"] != "arrive":
            for (n, a, b) in o["rd"] + wr:
                d.update(j for (x, y, j) in wlast.get(n, []) if x < b and a < y)
            for (n, a, b) in wr:
                d.update(j for (x, y, j) in rlast.get(n, []) if x < b and a < y)
        for out in o["outs"]:
            n, a, b = spans(out)[0]
            if out[6] == 1 and out[3] - out[2] == 128:
                wlast[n] = [e for e in wlast.get(n, []) if not (a <= e[0] and e[1] <= b)]
                rlast[n] = [e for e in rlast.get(n, []) if not (a <= e[0] and e[1] <= b)]
            wlast.setdefault(n, []).append((a, b, i))
        for (n, a, b) in o["rd"]:
            rlast.setdefault(n, []).append((a, b, i))
        d.discard(i)
        o["deps"] = d
        o["banks"] = sorted(set(n for (n, a, b) in o["rd"] + wr if SCRATCH[n][0] == "psum"))
    return ops


def order(ops):
    seq = [int(ORDER[k:k + 2], 36) for k in range(0, len(ORDER), 2)] or list(range(len(ops)))
    assert sorted(seq) == list(range(len(ops)))
    user, gone = {}, set()
    for i in seq:
        o = ops[i]
        assert o["deps"] <= gone
        gone.add(i)
        o["all"] = set(o["deps"])
        for b in o["banks"]:
            o["all"].update(j for e, j in user.get(b, {}).items() if e != o["eng"])
            user.setdefault(b, {})[o["eng"]] = i
    return seq


def rank_program(g, core, T, topo):
    r = T.rank_of(core)
    if r is None:
        return
    ops = plan(r)
    seq = order(ops)
    queue = {"V": g.vector, "A": g.scalar, "P": g.tensor, "G": g, "S": g.sync}
    peers = [c for c in T.cores if c != core]
    ids = [DstId(rid=topo.addr(c)[0], pnc=topo.addr(c)[1]) for c in peers]
    engines = [e for e in topo.engines(core, peers[0]) if all(e in topo.engines(core, c) for c in peers)]

    def ap(a):
        if not isview(a):
            return a
        if a[0] == "i":
            return ap(a[1]).indirect(ap(a[2]))
        return T[a[1]][a[2]:a[3], a[4]:a[5]:a[6]] if a[6] > 1 else T[a[1]][a[2]:a[3], a[4]:a[5]]

    def needs(o):
        if "loose" in o:
            return []
        return [j for j in o["all"] if ops[j]["call"] != "send" and not (o["eng"] == "P" and ops[j]["eng"] == "P")]

    pos = {i: k for k, i in enumerate(seq)}
    wanted = set()
    seen = {e: {} for e in queue}
    waits = {}
    for i in seq:
        o = ops[i]
        if o["eng"] == "X":
            continue
        last = {}
        for j in needs(o):
            key = ops[j]["sem"] if "sem" in ops[j] else "c" + ops[j]["eng"]
            if key not in last or pos[j] > pos[last[key]]:
                last[key] = j
        waits[i] = []
        for key in sorted(last):
            j = last[key]
            if seen[o["eng"]].get(key, -1) < pos[j]:
                seen[o["eng"]][key] = pos[j]
                waits[i].append((key, j))
                wanted.add(j)
    value = {}
    total = {}
    for i in seq:
        o = ops[i]
        if o["eng"] == "X":
            value[i] = o["val"]
            continue
        q = queue[o["eng"]]
        for key, j in waits[i]:
            q.wait_ge(T.sem[key], value[j])
        c, a = o["call"], o["args"]
        if c == "send":
            per = len(engines) // len(a)
            trs = []
            for k, piece in enumerate(a):
                m = sum(1 << e for e in engines[per * k:per * k + per])
                trs.append(RemoteDMATransfer(dst_ids=ids, dma_engine_mask=m, remote_sem=T.sem[o["sem"]],
                                             src=ap(piece), dsts=[ap(piece)] * len(ids)))
            g.remote_dma_fused(trs, local_sem=T.sem.sent)
            total["sent"] = total.get("sent", 0) + per * len(a)
            continue
        if c in ("load", "store", "cast"):
            if c == "load":
                ins = q.dma_start(ap(a[0]), T[o["src"]][:])
            elif c == "store":
                ins = q.dma_start(T[o["dst"]][:, a[0][4]:a[0][5]], ap(a[0]))
            else:
                ins = q.dma_start(ap(a[0]), ap(a[1]))
            ins.then_inc(T.sem[o["sem"]], 16)
            total[o["sem"]] = value[i] = total.get(o["sem"], 0) + 16
            continue
        x = [ap(y) for y in a]
        kw = {k: ap(y) for k, y in o["kw"].items()}
        if c == "matmul":
            for out, terms in a:
                for k, (lhs, rhs) in enumerate(terms):
                    ins = q.matmul(ap(out), ap(lhs), ap(rhs), k == 0, k == len(terms) - 1)
        elif c == "tensor_scalar":
            ins = q.tensor_scalar(*x)
        elif c == "tensor_tensor":
            ins = q.tensor_tensor(*x)
        elif c == "tensor_copy":
            ins = q.tensor_copy(*x)
        elif c == "memset":
            ins = q.memset(*x)
        elif c == "tensor_tensor_scan":
            ins = q.tensor_tensor_scan(*x)
        elif c == "activation":
            ins = q.activation(*x, **kw)
        elif c == "iota":
            ins = q.iota(*x, **kw)
        else:
            ins = q.affine_select(*x)
        if i in wanted:
            key = "c" + o["eng"]
            ins.then_inc(T.sem[key], 1)
            total[key] = value[i] = total.get(key, 0) + 1
    g.sync.wait_ge(T.sem.outs, total["outs"])
    g.wait_ge(T.sem.sent, total["sent"])
